import numpy as np
import ml_dtypes


def mxq(x, axis, fmt="e4m3"):
    dtype, down = {"e4m3": (ml_dtypes.float8_e4m3fn, 7), "e5m2": (ml_dtypes.float8_e5m2, 14)}[fmt]
    v = np.moveaxis(np.asarray(x, np.float32).astype(ml_dtypes.bfloat16).astype(np.float64), axis, -1)
    blocks = v.reshape(v.shape[:-1] + (-1, 32))
    amax = np.abs(blocks).max(-1, keepdims=True)
    byte = np.maximum(np.where(amax > 0, np.frexp(amax)[1] - 1 + 127, 0) - down, 1)
    scale = np.exp2(byte - 127.0)
    codes = (blocks / scale).astype(np.float32).astype(dtype).astype(np.float64)
    return np.moveaxis((codes * scale).reshape(v.shape), -1, axis)


WIDE = False


def mx_kscale(k, group=512):
    if not WIDE:
        return np.ones(k)
    levels = np.array([10, -10, 5, -5, 0])
    if group != 512:
        return np.exp2(np.random.permutation(np.resize(levels, k // group))).repeat(group)
    if k % 512:
        return np.exp2(np.random.permutation(np.resize(levels, k // 32))).repeat(32)
    a = np.empty((k // 512, 16))
    for p in range(k // 512):
        a[p, :8] = np.random.permutation(np.resize(levels, 8))
        for g in range(8):
            far = levels[np.abs(levels - a[p, g]) >= 10]
            a[p, g + 8] = far[np.random.randint(len(far))]
    return np.exp2(a.ravel()).repeat(32)


def f64(x):
    return np.asarray(x).astype(np.float64)


H, D, N = 2, 256, 512


def setup_inputs():
    n = np.random.standard_normal
    s = mx_kscale(D, 0)[:, None]
    S = n((H, D, 128))
    S[:, :, 127] = np.random.uniform(0.5, 1.5, (H, D))
    return {
        "q": n((H, D, N)).astype(np.float32),
        "qa": (np.random.uniform(0.5, 2.0, (D, 1)) * s).astype(np.float32),
        "S": (S / s).astype(np.float32),
        "og": n((H, N, 128)).astype(np.float32),
    }


def reference(q, qa, S, og):
    fq = (np.square(f64(q)) + 0.125) * f64(qa)
    y = mxq(fq, 1, "e4m3").transpose(0, 2, 1) @ mxq(f64(S), 1, "e4m3")
    y = y / y[:, :, 127:128]
    y = y / (1.0 + np.exp(-f64(og)))
    return y

@@ -1,0 +1,158 @@
+from contextlib import ExitStack
+
+import concourse.mybir as mybir
+
+H, D, N, E = 2, 256, 512, 128
+FLOPS = 2 * H * N * D * E
+
+F32 = mybir.dt.float32
+BF16 = mybir.dt.bfloat16
+U32 = mybir.dt.uint32
+U8 = mybir.dt.uint8
+FP8X4 = mybir.dt.float8_e4m3fn_x4
+ACT = mybir.ActivationFunctionType
+ALU = mybir.AluOpType
+
+P = 128
+PACK = 4
+ROWS = D // PACK
+DEAL = 2
+CHUNK = DEAL * P
+CHUNKS = N // CHUNK
+PIECES = 2
+PM = P // PIECES
+
+
+def tile_rows_read_sq_norm_gate_kernel(tc, q, qa, S, og, out):
+    nc = tc.nc
+    with ExitStack() as ctx:
+        sb = ctx.enter_context(tc.tile_pool(name="sb", bufs=1))
+        ps = ctx.enter_context(tc.psum_pool(name="ps", bufs=1))
+        ctx.enter_context(tc.manual_schedule())
+
+        q_rows = q.rearrange("h (p j) n -> (h p) j n", j=PACK)
+        og_rows = og.rearrange("h (c m r) e -> c m h (r e)", c=CHUNKS, r=DEAL)
+        out_rows = out.rearrange("h (c m r) e -> c h m (r e)", c=CHUNKS, r=DEAL)
+
+        q_sb = [sb.tile([P, PACK, CHUNK], F32, name=f"q{c}") for c in range(CHUNKS)]
+        og_sb = [sb.tile([P, H, DEAL * E], F32, name=f"og{c}") for c in range(CHUNKS)]
+        gate = [sb.tile([P, H, DEAL * E], F32, name=f"gate{c}") for c in range(CHUNKS)]
+        s_sb = sb.tile([P, PACK, E], F32)
+        qa_sb = sb.tile([P, PACK], F32)
+        s_bf = sb.tile([P, E, PACK], BF16, align_bytes=64)
+        s_codes = sb.tile([P, E], U32, align_bytes=64)
+        s_scales = sb.tile([P, E], U8, align_bytes=64)
+        sq = [[sb.tile([P, DEAL, PM, PACK], F32, name=f"sq{c}_{k}") for k in range(PIECES)] for c in range(CHUNKS)]
+        fq = [sb.tile([P, DEAL, P, PACK], BF16, align_bytes=64, name=f"fq{c}") for c in range(CHUNKS)]
+        q_codes = [sb.tile([P, CHUNK], U32, align_bytes=64, name=f"qc{c}") for c in range(CHUNKS)]
+        q_scales = [sb.tile([P, CHUNK], U8, align_bytes=64, name=f"qs{c}") for c in range(CHUNKS)]
+        y = [[ps.tile([P, DEAL, E], F32, name=f"y{c}_{h}") for h in range(H)] for c in range(CHUNKS)]
+        rcp = [[sb.tile([P, DEAL], F32, name=f"rcp{c}_{h}") for h in range(H)] for c in range(CHUNKS)]
+        res = [[sb.tile([P, DEAL * E], F32, name=f"res{c}_{h}") for h in range(H)] for c in range(CHUNKS)]
+        warm_in = sb.tile([P, 1], F32)
+        warm_out = sb.tile([P, 1], F32)
+
+        nc.sync.dma_start(out=q_sb[0][:], in_=q_rows[:, :, 0:CHUNK])
+        for h in range(H):
+            nc.scalar.dma_start(out=qa_sb[h * ROWS:(h + 1) * ROWS, :], in_=qa.rearrange("(p j) o -> p (j o)", j=PACK))
+        nc.sync.dma_start(out=s_sb[:], in_=S.rearrange("h (p j) e -> (h p) j e", j=PACK))
+        nc.sync.dma_start(out=q_sb[1][:], in_=q_rows[:, :, CHUNK:2 * CHUNK])
+        for c in range(CHUNKS):
+            nc.sync.dma_start(out=og_sb[c][:], in_=og_rows[c])
+
+        nc.vector.memset(warm_in[:], 0.0)
+        nc.scalar.activation(out=warm_out[:], in_=warm_in[:], func=ACT.Sigmoid)
+
+        def square(c, k):
+            cols = q_sb[c][:, :, k * DEAL * PM:(k + 1) * DEAL * PM]
+            nc.scalar.activation(
+                out=sq[c][k][:].rearrange("p r m j -> p m j r"),
+                in_=cols.rearrange("p j (m r) -> p m j r", r=DEAL),
+                func=ACT.Square,
+            )
+
+        def feature_map(c, k):
+            nc.vector.scalar_tensor_tensor(
+                out=fq[c][:, :, k * PM:(k + 1) * PM, :].rearrange("p r m j -> p r (m j)"),
+                in0=sq[c][k][:].rearrange("p r m j -> p (r m) j"),
+                scalar=0.125,
+                in1=qa_sb[:].unsqueeze(1).to_broadcast([P, DEAL * PM, PACK]),
+                op0=ALU.add,
+                op1=ALU.mult,
+            )
+
+        def quantize_q(c):
+            nc.vector.quantize_mx(
+                out=q_codes[c][:].bitcast(FP8X4),
+                scales=q_scales[c][:],
+                in_=fq[c][:].rearrange("p r m j -> p (r m j)"),
+            )
+
+        def multiply(c):
+            for h in range(H):
+                rows = slice(h * ROWS, (h + 1) * ROWS)
+                for r in range(DEAL):
+                    cols = slice(r * P, (r + 1) * P)
+                    nc.tensor.matmul_mx(
+                        out=y[c][h][:, r, :],
+                        lhsT=q_codes[c][rows, cols].bitcast(FP8X4),
+                        lhsT_scale=q_scales[c][rows, cols],
+                        rhs=s_codes[rows, :].bitcast(FP8X4),
+                        rhs_scale=s_scales[rows, :],
+                        start=True,
+                        stop=True,
+                    )
+
+        def sigmoid(c, h):
+            nc.scalar.activation(out=gate[c][:, h, :], in_=og_sb[c][:, h, :], func=ACT.Sigmoid)
+
+        def denominators(c, h):
+            nc.vector.reciprocal(out=rcp[c][h][:], in_=y[c][h][:, :, E - 1])
+
+        def finish(c, h, r):
+            nc.vector.scalar_tensor_tensor(
+                out=res[c][h][:, r * E:(r + 1) * E],
+                in0=y[c][h][:, r, :],
+                scalar=rcp[c][h][:, r:r + 1],
+                in1=gate[c][:, h, r * E:(r + 1) * E],
+                op0=ALU.mult,
+                op1=ALU.mult,
+            )
+
+        def store(c, h):
+            nc.sync.dma_start(out=out_rows[c, h], in_=res[c][h][:])
+
+        square(0, 0)
+        square(0, 1)
+        nc.vector.tensor_copy(
+            out=s_bf[:].rearrange("p (a i) j -> p a j i", i=2),
+            in_=s_sb[:].rearrange("p j (a i) -> p a j i", i=2),
+        )
+        feature_map(0, 0)
+        feature_map(0, 1)
+        nc.vector.quantize_mx(out=s_codes[:].bitcast(FP8X4), scales=s_scales[:], in_=s_bf[:].rearrange("p e j -> p (e j)"))
+        quantize_q(0)
+        multiply(0)
+        square(1, 0)
+        square(1, 1)
+        for c in range(CHUNKS):
+            for h in range(H):
+                sigmoid(c, h)
+        feature_map(1, 0)
+        denominators(0, 0)
+        denominators(0, 1)
+        feature_map(1, 1)
+        finish(0, 0, 0)
+        quantize_q(1)
+        multiply(1)
+        finish(0, 0, 1)
+        store(0, 0)
+        finish(0, 1, 0)
+        finish(0, 1, 1)
+        store(0, 1)
+        denominators(1, 0)
+        denominators(1, 1)
+        for h in range(H):
+            for r in range(DEAL):
+                finish(1, h, r)
+            store(1, h)

@@ -16,11 +16,9 @@ ALU = mybir.AluOpType
 P = 128
 PACK = 4
 ROWS = D // PACK
-DEAL = 2
-CHUNK = DEAL * P
-CHUNKS = N // CHUNK
-PIECES = 2
-PM = P // PIECES
+HALF = N // 2
+PAIR = 2
+PIECES = [32,48,48]
 
 
 def tile_rows_read_sq_norm_gate_kernel(tc, q, qa, S, og, out):
@@ -31,128 +29,218 @@ def tile_rows_read_sq_norm_gate_kernel(tc, q, qa, S, og, out):
         ctx.enter_context(tc.manual_schedule())
 
         q_rows = q.rearrange("h (p j) n -> (h p) j n", j=PACK)
-        og_rows = og.rearrange("h (c m r) e -> c m h (r e)", c=CHUNKS, r=DEAL)
-        out_rows = out.rearrange("h (c m r) e -> c h m (r e)", c=CHUNKS, r=DEAL)
+        og_a_rows = og[:, 0:HALF, :].rearrange("h (m r) e -> m h (r e)", r=PAIR)
+        out_a_rows = out[:, 0:HALF, :].rearrange("h (m r) e -> h m (r e)", r=PAIR)
+        og_b_rows = og[:, HALF:N, :].rearrange("h (r m) e -> r m h e", r=PAIR)
+        out_b_rows = out[:, HALF:N, :].rearrange("h (r m) e -> r m h e", r=PAIR)
 
-        q_sb = [sb.tile([P, PACK, CHUNK], F32, name=f"q{c}") for c in range(CHUNKS)]
-        og_sb = [sb.tile([P, H, DEAL * E], F32, name=f"og{c}") for c in range(CHUNKS)]
-        gate = [sb.tile([P, H, DEAL * E], F32, name=f"gate{c}") for c in range(CHUNKS)]
+        q_sb = [sb.tile([P, PACK, HALF], F32, name=f"q{c}") for c in range(2)]
+        og_a = sb.tile([P, H, PAIR * E], F32)
+        gate_a = sb.tile([P, H, PAIR * E], F32)
+        og_b = [sb.tile([P, H, E], F32, name=f"ogb{r}") for r in range(PAIR)]
+        gate_b = [sb.tile([P, H, E], F32, name=f"gateb{r}") for r in range(PAIR)]
         s_sb = sb.tile([P, PACK, E], F32)
         qa_sb = sb.tile([P, PACK], F32)
         s_bf = sb.tile([P, E, PACK], BF16, align_bytes=64)
         s_codes = sb.tile([P, E], U32, align_bytes=64)
         s_scales = sb.tile([P, E], U8, align_bytes=64)
-        sq = [[sb.tile([P, DEAL, PM, PACK], F32, name=f"sq{c}_{k}") for k in range(PIECES)] for c in range(CHUNKS)]
-        fq = [sb.tile([P, DEAL, P, PACK], BF16, align_bytes=64, name=f"fq{c}") for c in range(CHUNKS)]
-        q_codes = [sb.tile([P, CHUNK], U32, align_bytes=64, name=f"qc{c}") for c in range(CHUNKS)]
-        q_scales = [sb.tile([P, CHUNK], U8, align_bytes=64, name=f"qs{c}") for c in range(CHUNKS)]
-        y = [[ps.tile([P, DEAL, E], F32, name=f"y{c}_{h}") for h in range(H)] for c in range(CHUNKS)]
-        rcp = [[sb.tile([P, DEAL], F32, name=f"rcp{c}_{h}") for h in range(H)] for c in range(CHUNKS)]
-        res = [[sb.tile([P, DEAL * E], F32, name=f"res{c}_{h}") for h in range(H)] for c in range(CHUNKS)]
+        sq_a = [sb.tile([P, PAIR, width, PACK], F32, name=f"sqa{k}") for k, width in enumerate(PIECES)]
+        sq_b = [sb.tile([P, P, PACK], F32, name=f"sqb{r}") for r in range(PAIR)]
+        fq_a = sb.tile([P, PAIR, P, PACK], BF16, align_bytes=64)
+        fq_b = [sb.tile([P, P, PACK], BF16, align_bytes=64, name=f"fqb{r}") for r in range(PAIR)]
+        codes_a = sb.tile([P, HALF], U32, align_bytes=64)
+        scales_a = sb.tile([P, HALF], U8, align_bytes=64)
+        codes_b = [sb.tile([P, P], U32, align_bytes=64, name=f"qcb{r}") for r in range(PAIR)]
+        scales_b = [sb.tile([P, P], U8, align_bytes=64, name=f"qsb{r}") for r in range(PAIR)]
+        y_a = [ps.tile([P, PAIR, E], F32, name=f"ya{h}") for h in range(H)]
+        y_b = [[ps.tile([P, E], F32, name=f"yb{r}_{h}") for h in range(H)] for r in range(PAIR)]
+        rcp_a = [sb.tile([P, PAIR], F32, name=f"rcpa{h}") for h in range(H)]
+        rcp_b = [[sb.tile([P, 1], F32, name=f"rcpb{r}_{h}") for h in range(H)] for r in range(PAIR)]
+        res_a = [sb.tile([P, PAIR * E], F32, name=f"resa{h}") for h in range(H)]
+        res_b = [sb.tile([P, H, E], F32, name=f"resb{r}") for r in range(PAIR)]
+        normed = sb.tile([P, PAIR * E], F32)
         warm_in = sb.tile([P, 1], F32)
         warm_out = sb.tile([P, 1], F32)
 
-        nc.sync.dma_start(out=q_sb[0][:], in_=q_rows[:, :, 0:CHUNK])
-        for h in range(H):
-            nc.scalar.dma_start(out=qa_sb[h * ROWS:(h + 1) * ROWS, :], in_=qa.rearrange("(p j) o -> p (j o)", j=PACK))
-        nc.sync.dma_start(out=s_sb[:], in_=S.rearrange("h (p j) e -> (h p) j e", j=PACK))
-        nc.sync.dma_start(out=q_sb[1][:], in_=q_rows[:, :, CHUNK:2 * CHUNK])
-        for c in range(CHUNKS):
-            nc.sync.dma_start(out=og_sb[c][:], in_=og_rows[c])
+        def load_q(c):
+            nc.sync.dma_start(out=q_sb[c][:], in_=q_rows[:, :, c * HALF:(c + 1) * HALF])
+
+        def load_qa(engine):
+            for h in range(H):
+                engine.dma_start(out=qa_sb[h * ROWS:(h + 1) * ROWS, :], in_=qa.rearrange("(p j) o -> p (j o)", j=PACK))
+
+        def load_s():
+            nc.sync.dma_start(out=s_sb[:], in_=S.rearrange("h (p j) e -> (h p) j e", j=PACK))
+
+        def load_og_a():
+            nc.sync.dma_start(out=og_a[:], in_=og_a_rows)
+
+        def load_og_b(r):
+            nc.sync.dma_start(out=og_b[r][:], in_=og_b_rows[r])
+
+        load_q(0)
+        load_qa(nc.sync)
+        load_s()
+        load_q(1)
+        load_og_a()
+        load_og_b(0)
+        load_og_b(1)
 
         nc.vector.memset(warm_in[:], 0.0)
         nc.scalar.activation(out=warm_out[:], in_=warm_in[:], func=ACT.Sigmoid)
 
-        def square(c, k):
-            cols = q_sb[c][:, :, k * DEAL * PM:(k + 1) * DEAL * PM]
+        def square_a(k):
+            first = sum(PIECES[:k])
+            cols = q_sb[0][:, :, PAIR * first:PAIR * (first + PIECES[k])]
             nc.scalar.activation(
-                out=sq[c][k][:].rearrange("p r m j -> p m j r"),
-                in_=cols.rearrange("p j (m r) -> p m j r", r=DEAL),
+                out=sq_a[k][:].rearrange("p r m j -> p m j r"),
+                in_=cols.rearrange("p j (m r) -> p m j r", r=PAIR),
                 func=ACT.Square,
             )
 
-        def feature_map(c, k):
+        def square_b(r):
+            nc.scalar.activation(
+                out=sq_b[r][:].rearrange("p (a i) j -> p a j i", i=PAIR),
+                in_=q_sb[1][:, :, r * P:(r + 1) * P].rearrange("p j (a i) -> p a j i", i=PAIR),
+                func=ACT.Square,
+            )
+
+        def feature_map(dst, squares, columns):
             nc.vector.scalar_tensor_tensor(
-                out=fq[c][:, :, k * PM:(k + 1) * PM, :].rearrange("p r m j -> p r (m j)"),
-                in0=sq[c][k][:].rearrange("p r m j -> p (r m) j"),
+                out=dst,
+                in0=squares,
                 scalar=0.125,
-                in1=qa_sb[:].unsqueeze(1).to_broadcast([P, DEAL * PM, PACK]),
+                in1=qa_sb[:].unsqueeze(1).to_broadcast([P, columns, PACK]),
                 op0=ALU.add,
                 op1=ALU.mult,
             )
 
-        def quantize_q(c):
-            nc.vector.quantize_mx(
-                out=q_codes[c][:].bitcast(FP8X4),
-                scales=q_scales[c][:],
-                in_=fq[c][:].rearrange("p r m j -> p (r m j)"),
+        def map_a(k):
+            first = sum(PIECES[:k])
+            feature_map(
+                fq_a[:, :, first:first + PIECES[k], :].rearrange("p r m j -> p r (m j)"),
+                sq_a[k][:].rearrange("p r m j -> p (r m) j"),
+                PAIR * PIECES[k],
             )
 
-        def multiply(c):
-            for h in range(H):
-                rows = slice(h * ROWS, (h + 1) * ROWS)
-                for r in range(DEAL):
-                    cols = slice(r * P, (r + 1) * P)
-                    nc.tensor.matmul_mx(
-                        out=y[c][h][:, r, :],
-                        lhsT=q_codes[c][rows, cols].bitcast(FP8X4),
-                        lhsT_scale=q_scales[c][rows, cols],
-                        rhs=s_codes[rows, :].bitcast(FP8X4),
-                        rhs_scale=s_scales[rows, :],
-                        start=True,
-                        stop=True,
-                    )
+        def map_b(r):
+            feature_map(fq_b[r][:], sq_b[r][:], P)
 
-        def sigmoid(c, h):
-            nc.scalar.activation(out=gate[c][:, h, :], in_=og_sb[c][:, h, :], func=ACT.Sigmoid)
+        def quantize(codes, scales, values):
+            nc.vector.quantize_mx(out=codes[:].bitcast(FP8X4), scales=scales[:], in_=values)
 
-        def denominators(c, h):
-            nc.vector.reciprocal(out=rcp[c][h][:], in_=y[c][h][:, :, E - 1])
+        def quantize_a():
+            quantize(codes_a, scales_a, fq_a[:].rearrange("p r m j -> p (r m j)"))
 
-        def finish(c, h, r):
-            nc.vector.scalar_tensor_tensor(
-                out=res[c][h][:, r * E:(r + 1) * E],
-                in0=y[c][h][:, r, :],
-                scalar=rcp[c][h][:, r:r + 1],
-                in1=gate[c][:, h, r * E:(r + 1) * E],
-                op0=ALU.mult,
-                op1=ALU.mult,
+        def quantize_b(r):
+            quantize(codes_b[r], scales_b[r], fq_b[r][:].rearrange("p m j -> p (m j)"))
+
+        def quantize_s():
+            quantize(s_codes, s_scales, s_bf[:].rearrange("p e j -> p (e j)"))
+
+        def multiply(dst, h, codes, scales, cols):
+            rows = slice(h * ROWS, (h + 1) * ROWS)
+            nc.tensor.matmul_mx(
+                out=dst,
+                lhsT=codes[rows, cols].bitcast(FP8X4),
+                lhsT_scale=scales[rows, cols],
+                rhs=s_codes[rows, :].bitcast(FP8X4),
+                rhs_scale=s_scales[rows, :],
+                start=True,
+                stop=True,
             )
 
-        def store(c, h):
-            nc.sync.dma_start(out=out_rows[c, h], in_=res[c][h][:])
+        def multiply_a():
+            for r in range(PAIR):
+                for h in range(H):
+                    multiply(y_a[h][:, r, :], h, codes_a, scales_a, slice(r * P, (r + 1) * P))
 
-        square(0, 0)
-        square(0, 1)
-        nc.vector.tensor_copy(
-            out=s_bf[:].rearrange("p (a i) j -> p a j i", i=2),
-            in_=s_sb[:].rearrange("p j (a i) -> p a j i", i=2),
-        )
-        feature_map(0, 0)
-        feature_map(0, 1)
-        nc.vector.quantize_mx(out=s_codes[:].bitcast(FP8X4), scales=s_scales[:], in_=s_bf[:].rearrange("p e j -> p (e j)"))
-        quantize_q(0)
-        multiply(0)
-        square(1, 0)
-        square(1, 1)
-        for c in range(CHUNKS):
+        def multiply_b(r):
             for h in range(H):
-                sigmoid(c, h)
-        feature_map(1, 0)
-        denominators(0, 0)
-        denominators(0, 1)
-        feature_map(1, 1)
-        finish(0, 0, 0)
-        quantize_q(1)
-        multiply(1)
-        finish(0, 0, 1)
-        store(0, 0)
-        finish(0, 1, 0)
-        finish(0, 1, 1)
-        store(0, 1)
-        denominators(1, 0)
-        denominators(1, 1)
-        for h in range(H):
-            for r in range(DEAL):
-                finish(1, h, r)
-            store(1, h)
+                multiply(y_b[r][h][:], h, codes_b[r], scales_b[r], slice(0, P))
+
+        def sigmoid_a(h):
+            nc.scalar.activation(out=gate_a[:, h, :], in_=og_a[:, h, :], func=ACT.Sigmoid)
+
+        def sigmoid_b(r):
+            nc.scalar.activation(out=gate_b[r][:], in_=og_b[r][:], func=ACT.Sigmoid)
+
+        def rcp_of_a(h):
+            nc.vector.reciprocal(out=rcp_a[h][:], in_=y_a[h][:, :, E - 1])
+
+        def rcp_of_b(r, h):
+            nc.vector.reciprocal(out=rcp_b[r][h][:], in_=y_b[r][h][:, E - 1:E])
+
+        def finish(dst, sums, rcp, gate):
+            nc.vector.scalar_tensor_tensor(out=dst, in0=sums, scalar=rcp, in1=gate, op0=ALU.mult, op1=ALU.mult)
+
+        def finish_a(h, r):
+            cols = slice(r * E, (r + 1) * E)
+            finish(res_a[h][:, cols], y_a[h][:, r, :], rcp_a[h][:, r:r + 1], gate_a[:, h, cols])
+
+        def finish_b(r, h):
+            finish(res_b[r][:, h, :], y_b[r][h][:], rcp_b[r][h][:], gate_b[r][:, h, :])
+
+        def normalise_a(h, r):
+            nc.scalar.activation(out=normed[:, r * E:(r + 1) * E], in_=y_a[h][:, r, :], func=ACT.Copy, scale=rcp_a[h][:, r:r + 1])
+
+        def gate_of_a(h, r):
+            cols = slice(r * E, (r + 1) * E)
+            nc.gpsimd.tensor_tensor(out=res_a[h][:, cols], in0=normed[:, cols], in1=gate_a[:, h, cols], op=ALU.mult)
+
+        def store_a(h):
+            nc.sync.dma_start(out=out_a_rows[h], in_=res_a[h][:])
+
+        def store_b(r):
+            nc.sync.dma_start(out=out_b_rows[r], in_=res_b[r][:])
+
+        def store_b_head(engine, r, h):
+            engine.dma_start(out=out_b_rows[r][:, h, :], in_=res_b[r][:, h, :])
+
+        def pack_s(copy):
+            copy(
+                out=s_bf[:].rearrange("p (a i) j -> p a j i", i=PAIR),
+                in_=s_sb[:].rearrange("p j (a i) -> p a j i", i=PAIR),
+            )
+
+        square_a(0)
+        square_a(1)
+        square_a(2)
+        pack_s(nc.scalar.copy)
+        square_b(0)
+        square_b(1)
+        sigmoid_a(0)
+        sigmoid_a(1)
+        sigmoid_b(0)
+        sigmoid_b(1)
+        map_a(0)
+        map_a(1)
+        map_a(2)
+        quantize_s()
+        quantize_a()
+        multiply_a()
+        map_b(0)
+        map_b(1)
+        quantize_b(0)
+        multiply_b(0)
+        rcp_of_a(0)
+        rcp_of_a(1)
+        quantize_b(1)
+        multiply_b(1)
+        finish_a(0, 0)
+        finish_a(0, 1)
+        store_a(0)
+        rcp_of_b(0, 0)
+        rcp_of_b(0, 1)
+        finish_a(1, 0)
+        finish_a(1, 1)
+        store_a(1)
+        rcp_of_b(1, 0)
+        rcp_of_b(1, 1)
+        finish_b(0, 0)
+        finish_b(0, 1)
+        store_b(0)
+        finish_b(1, 0)
+        store_b_head(nc.sync, 1, 0)
+        finish_b(1, 1)
+        store_b_head(nc.scalar, 1, 1)

@@ -34,7 +34,8 @@ def tile_rows_read_sq_norm_gate_kernel(tc, q, qa, S, og, out):
         og_b_rows = og[:, HALF:N, :].rearrange("h (r m) e -> r m h e", r=PAIR)
         out_b_rows = out[:, HALF:N, :].rearrange("h (r m) e -> r m h e", r=PAIR)
 
-        q_sb = [sb.tile([P, PACK, HALF], F32, name=f"q{c}") for c in range(2)]
+        q_sb = [sb.tile([P, PACK, HALF], F32, name=f"q{c}") for c in range(1)]
+        q_b = [sb.tile([P, PACK, P], F32, name=f"qb{r}") for r in range(PAIR)]
         og_a = sb.tile([P, H, PAIR * E], F32)
         gate_a = sb.tile([P, H, PAIR * E], F32)
         og_b = [sb.tile([P, H, E], F32, name=f"ogb{r}") for r in range(PAIR)]
@@ -58,12 +59,14 @@ def tile_rows_read_sq_norm_gate_kernel(tc, q, qa, S, og, out):
         rcp_b = [[sb.tile([P, 1], F32, name=f"rcpb{r}_{h}") for h in range(H)] for r in range(PAIR)]
         res_a = [sb.tile([P, PAIR * E], F32, name=f"resa{h}") for h in range(H)]
         res_b = [sb.tile([P, H, E], F32, name=f"resb{r}") for r in range(PAIR)]
-        normed = sb.tile([P, PAIR * E], F32)
         warm_in = sb.tile([P, 1], F32)
         warm_out = sb.tile([P, 1], F32)
 
         def load_q(c):
             nc.sync.dma_start(out=q_sb[c][:], in_=q_rows[:, :, c * HALF:(c + 1) * HALF])
+
+        def load_q_b(r):
+            nc.sync.dma_start(out=q_b[r][:], in_=q_rows[:, :, HALF + r * P:HALF + (r + 1) * P])
 
         def load_qa(engine):
             for h in range(H):
@@ -81,7 +84,8 @@ def tile_rows_read_sq_norm_gate_kernel(tc, q, qa, S, og, out):
         load_q(0)
         load_qa(nc.sync)
         load_s()
-        load_q(1)
+        load_q_b(0)
+        load_q_b(1)
         load_og_a()
         load_og_b(0)
         load_og_b(1)
@@ -98,10 +102,10 @@ def tile_rows_read_sq_norm_gate_kernel(tc, q, qa, S, og, out):
                 func=ACT.Square,
             )
 
-        def square_b(r):
+        def square_b(r, lo=0, hi=P):
             nc.scalar.activation(
-                out=sq_b[r][:].rearrange("p (a i) j -> p a j i", i=PAIR),
-                in_=q_sb[1][:, :, r * P:(r + 1) * P].rearrange("p j (a i) -> p a j i", i=PAIR),
+                out=sq_b[r][:, lo:hi, :].rearrange("p (a i) j -> p a j i", i=PAIR),
+                in_=q_b[r][:, :, lo:hi].rearrange("p j (a i) -> p a j i", i=PAIR),
                 func=ACT.Square,
             )
 
@@ -123,8 +127,8 @@ def tile_rows_read_sq_norm_gate_kernel(tc, q, qa, S, og, out):
                 PAIR * PIECES[k],
             )
 
-        def map_b(r):
-            feature_map(fq_b[r][:], sq_b[r][:], P)
+        def map_b(r, lo=0, hi=P):
+            feature_map(fq_b[r][:, lo:hi, :], sq_b[r][:, lo:hi, :], hi - lo)
 
         def quantize(codes, scales, values):
             nc.vector.quantize_mx(out=codes[:].bitcast(FP8X4), scales=scales[:], in_=values)
@@ -181,15 +185,8 @@ def tile_rows_read_sq_norm_gate_kernel(tc, q, qa, S, og, out):
         def finish_b(r, h):
             finish(res_b[r][:, h, :], y_b[r][h][:], rcp_b[r][h][:], gate_b[r][:, h, :])
 
-        def normalise_a(h, r):
-            nc.scalar.activation(out=normed[:, r * E:(r + 1) * E], in_=y_a[h][:, r, :], func=ACT.Copy, scale=rcp_a[h][:, r:r + 1])
-
-        def gate_of_a(h, r):
-            cols = slice(r * E, (r + 1) * E)
-            nc.gpsimd.tensor_tensor(out=res_a[h][:, cols], in0=normed[:, cols], in1=gate_a[:, h, cols], op=ALU.mult)
-
-        def store_a(h):
-            nc.sync.dma_start(out=out_a_rows[h], in_=res_a[h][:])
+        def store_a(engine, h):
+            engine.dma_start(out=out_a_rows[h], in_=res_a[h][:])
 
         def store_b(r):
             nc.sync.dma_start(out=out_b_rows[r], in_=res_b[r][:])
@@ -208,7 +205,8 @@ def tile_rows_read_sq_norm_gate_kernel(tc, q, qa, S, og, out):
         square_a(2)
         pack_s(nc.scalar.copy)
         square_b(0)
-        square_b(1)
+        square_b(1, 0, 64)
+        square_b(1, 64, 128)
         sigmoid_a(0)
         sigmoid_a(1)
         sigmoid_b(0)
@@ -220,21 +218,22 @@ def tile_rows_read_sq_norm_gate_kernel(tc, q, qa, S, og, out):
         quantize_a()
         multiply_a()
         map_b(0)
-        map_b(1)
+        map_b(1, 0, 64)
         quantize_b(0)
         multiply_b(0)
+        map_b(1, 64, 128)
         rcp_of_a(0)
         rcp_of_a(1)
         quantize_b(1)
         multiply_b(1)
         finish_a(0, 0)
         finish_a(0, 1)
-        store_a(0)
+        store_a(nc.sync, 0)
         rcp_of_b(0, 0)
         rcp_of_b(0, 1)
         finish_a(1, 0)
         finish_a(1, 1)
-        store_a(1)
+        store_a(nc.sync, 1)
         rcp_of_b(1, 0)
         rcp_of_b(1, 1)
         finish_b(0, 0)

@@ -34,8 +34,7 @@ def tile_rows_read_sq_norm_gate_kernel(tc, q, qa, S, og, out):
         og_b_rows = og[:, HALF:N, :].rearrange("h (r m) e -> r m h e", r=PAIR)
         out_b_rows = out[:, HALF:N, :].rearrange("h (r m) e -> r m h e", r=PAIR)
 
-        q_sb = [sb.tile([P, PACK, HALF], F32, name=f"q{c}") for c in range(1)]
-        q_b = [sb.tile([P, PACK, P], F32, name=f"qb{r}") for r in range(PAIR)]
+        q_sb = [sb.tile([P, PACK, HALF], F32, name=f"q{c}") for c in range(2)]
         og_a = sb.tile([P, H, PAIR * E], F32)
         gate_a = sb.tile([P, H, PAIR * E], F32)
         og_b = [sb.tile([P, H, E], F32, name=f"ogb{r}") for r in range(PAIR)]
@@ -53,10 +52,12 @@ def tile_rows_read_sq_norm_gate_kernel(tc, q, qa, S, og, out):
         scales_a = sb.tile([P, HALF], U8, align_bytes=64)
         codes_b = [sb.tile([P, P], U32, align_bytes=64, name=f"qcb{r}") for r in range(PAIR)]
         scales_b = [sb.tile([P, P], U8, align_bytes=64, name=f"qsb{r}") for r in range(PAIR)]
-        y_a = [ps.tile([P, PAIR, E], F32, name=f"ya{h}") for h in range(H)]
-        y_b = [[ps.tile([P, E], F32, name=f"yb{r}_{h}") for h in range(H)] for r in range(PAIR)]
-        rcp_a = [sb.tile([P, PAIR], F32, name=f"rcpa{h}") for h in range(H)]
-        rcp_b = [[sb.tile([P, 1], F32, name=f"rcpb{r}_{h}") for h in range(H)] for r in range(PAIR)]
+        y_a = [ps.tile([P, PAIR + 1, E], F32, name=f"ya{h}") for h in range(H)]
+        y_last = [ps.tile([P, E], F32, name=f"yl{h}") for h in range(H)]
+        y_b = [[y_a[h][:, PAIR, :] for h in range(H)], [y_last[h][:] for h in range(H)]]
+        rcp_a = [sb.tile([P, PAIR + 1], F32, name=f"rcpa{h}") for h in range(H)]
+        rcp_last = [sb.tile([P, 1], F32, name=f"rcpl{h}") for h in range(H)]
+        rcp_b = [[rcp_a[h][:, PAIR:PAIR + 1] for h in range(H)], [rcp_last[h][:] for h in range(H)]]
         res_a = [sb.tile([P, PAIR * E], F32, name=f"resa{h}") for h in range(H)]
         res_b = [sb.tile([P, H, E], F32, name=f"resb{r}") for r in range(PAIR)]
         warm_in = sb.tile([P, 1], F32)
@@ -64,9 +65,6 @@ def tile_rows_read_sq_norm_gate_kernel(tc, q, qa, S, og, out):
 
         def load_q(c):
             nc.sync.dma_start(out=q_sb[c][:], in_=q_rows[:, :, c * HALF:(c + 1) * HALF])
-
-        def load_q_b(r):
-            nc.sync.dma_start(out=q_b[r][:], in_=q_rows[:, :, HALF + r * P:HALF + (r + 1) * P])
 
         def load_qa(engine):
             for h in range(H):
@@ -83,9 +81,8 @@ def tile_rows_read_sq_norm_gate_kernel(tc, q, qa, S, og, out):
 
         load_q(0)
         load_qa(nc.sync)
+        load_q(1)
         load_s()
-        load_q_b(0)
-        load_q_b(1)
         load_og_a()
         load_og_b(0)
         load_og_b(1)
@@ -105,7 +102,7 @@ def tile_rows_read_sq_norm_gate_kernel(tc, q, qa, S, og, out):
         def square_b(r, lo=0, hi=P):
             nc.scalar.activation(
                 out=sq_b[r][:, lo:hi, :].rearrange("p (a i) j -> p a j i", i=PAIR),
-                in_=q_b[r][:, :, lo:hi].rearrange("p j (a i) -> p a j i", i=PAIR),
+                in_=q_sb[1][:, :, r * P + lo:r * P + hi].rearrange("p j (a i) -> p a j i", i=PAIR),
                 func=ACT.Square,
             )
 
@@ -154,14 +151,12 @@ def tile_rows_read_sq_norm_gate_kernel(tc, q, qa, S, og, out):
                 stop=True,
             )
 
-        def multiply_a():
+        def multiply_a(h):
             for r in range(PAIR):
-                for h in range(H):
-                    multiply(y_a[h][:, r, :], h, codes_a, scales_a, slice(r * P, (r + 1) * P))
+                multiply(y_a[h][:, r, :], h, codes_a, scales_a, slice(r * P, (r + 1) * P))
 
-        def multiply_b(r):
-            for h in range(H):
-                multiply(y_b[r][h][:], h, codes_b[r], scales_b[r], slice(0, P))
+        def multiply_b(r, h):
+            multiply(y_b[r][h], h, codes_b[r], scales_b[r], slice(0, P))
 
         def sigmoid_a(h):
             nc.scalar.activation(out=gate_a[:, h, :], in_=og_a[:, h, :], func=ACT.Sigmoid)
@@ -173,7 +168,7 @@ def tile_rows_read_sq_norm_gate_kernel(tc, q, qa, S, og, out):
             nc.vector.reciprocal(out=rcp_a[h][:], in_=y_a[h][:, :, E - 1])
 
         def rcp_of_b(r, h):
-            nc.vector.reciprocal(out=rcp_b[r][h][:], in_=y_b[r][h][:, E - 1:E])
+            nc.vector.reciprocal(out=rcp_b[r][h], in_=y_b[r][h][:, E - 1:E])
 
         def finish(dst, sums, rcp, gate):
             nc.vector.scalar_tensor_tensor(out=dst, in0=sums, scalar=rcp, in1=gate, op0=ALU.mult, op1=ALU.mult)
@@ -183,7 +178,7 @@ def tile_rows_read_sq_norm_gate_kernel(tc, q, qa, S, og, out):
             finish(res_a[h][:, cols], y_a[h][:, r, :], rcp_a[h][:, r:r + 1], gate_a[:, h, cols])
 
         def finish_b(r, h):
-            finish(res_b[r][:, h, :], y_b[r][h][:], rcp_b[r][h][:], gate_b[r][:, h, :])
+            finish(res_b[r][:, h, :], y_b[r][h], rcp_b[r][h], gate_b[r][:, h, :])
 
         def store_a(engine, h):
             engine.dma_start(out=out_a_rows[h], in_=res_a[h][:])
@@ -203,42 +198,43 @@ def tile_rows_read_sq_norm_gate_kernel(tc, q, qa, S, og, out):
         square_a(0)
         square_a(1)
         square_a(2)
+        square_b(0, 0, 64)
+        square_b(0, 64, 128)
         pack_s(nc.scalar.copy)
-        square_b(0)
-        square_b(1, 0, 64)
-        square_b(1, 64, 128)
+        square_b(1)
         sigmoid_a(0)
-        sigmoid_a(1)
         sigmoid_b(0)
+        sigmoid_a(1)
         sigmoid_b(1)
         map_a(0)
         map_a(1)
         map_a(2)
-        quantize_s()
+        map_b(0, 0, 64)
+        map_b(0, 64, 128)
         quantize_a()
-        multiply_a()
-        map_b(0)
-        map_b(1, 0, 64)
+        quantize_s()
         quantize_b(0)
-        multiply_b(0)
-        map_b(1, 64, 128)
+        multiply_a(0)
+        multiply_b(0, 0)
+        multiply_a(1)
+        multiply_b(0, 1)
+        map_b(1)
         rcp_of_a(0)
-        rcp_of_a(1)
         quantize_b(1)
-        multiply_b(1)
+        multiply_b(1, 0)
+        multiply_b(1, 1)
         finish_a(0, 0)
+        rcp_of_a(1)
         finish_a(0, 1)
         store_a(nc.sync, 0)
-        rcp_of_b(0, 0)
-        rcp_of_b(0, 1)
-        finish_a(1, 0)
-        finish_a(1, 1)
-        store_a(nc.sync, 1)
-        rcp_of_b(1, 0)
-        rcp_of_b(1, 1)
         finish_b(0, 0)
         finish_b(0, 1)
         store_b(0)
+        finish_a(1, 0)
+        rcp_of_b(1, 0)
+        finish_a(1, 1)
+        store_a(nc.sync, 1)
+        rcp_of_b(1, 1)
         finish_b(1, 0)
         store_b_head(nc.sync, 1, 0)
         finish_b(1, 1)

from contextlib import ExitStack

import concourse.mybir as mybir

H, D, N, E = 2, 256, 512, 128
FLOPS = 2 * H * N * D * E

F32 = mybir.dt.float32
BF16 = mybir.dt.bfloat16
U32 = mybir.dt.uint32
U8 = mybir.dt.uint8
FP8X4 = mybir.dt.float8_e4m3fn_x4
ACT = mybir.ActivationFunctionType
ALU = mybir.AluOpType

P = 128
PACK = 4
ROWS = D // PACK
HALF = N // 2
PAIR = 2
PIECES = [32,48,48]


def tile_rows_read_sq_norm_gate_kernel(tc, q, qa, S, og, out):
    nc = tc.nc
    with ExitStack() as ctx:
        sb = ctx.enter_context(tc.tile_pool(name="sb", bufs=1))
        ps = ctx.enter_context(tc.psum_pool(name="ps", bufs=1))
        ctx.enter_context(tc.manual_schedule())

        q_rows = q.rearrange("h (p j) n -> (h p) j n", j=PACK)
        og_a_rows = og[:, 0:HALF, :].rearrange("h (m r) e -> m h (r e)", r=PAIR)
        out_a_rows = out[:, 0:HALF, :].rearrange("h (m r) e -> h m (r e)", r=PAIR)
        og_b_rows = og[:, HALF:N, :].rearrange("h (r m) e -> r m h e", r=PAIR)
        out_b_rows = out[:, HALF:N, :].rearrange("h (r m) e -> r m h e", r=PAIR)

        q_sb = [sb.tile([P, PACK, HALF], F32, name=f"q{c}") for c in range(2)]
        og_a = sb.tile([P, H, PAIR * E], F32)
        gate_a = sb.tile([P, H, PAIR * E], F32)
        og_b = [sb.tile([P, H, E], F32, name=f"ogb{r}") for r in range(PAIR)]
        gate_b = [sb.tile([P, H, E], F32, name=f"gateb{r}") for r in range(PAIR)]
        s_sb = sb.tile([P, PACK, E], F32)
        qa_sb = sb.tile([P, PACK], F32)
        s_bf = sb.tile([P, E, PACK], BF16, align_bytes=64)
        s_codes = sb.tile([P, E], U32, align_bytes=64)
        s_scales = sb.tile([P, E], U8, align_bytes=64)
        sq_a = [sb.tile([P, PAIR, width, PACK], F32, name=f"sqa{k}") for k, width in enumerate(PIECES)]
        sq_b = [sb.tile([P, P, PACK], F32, name=f"sqb{r}") for r in range(PAIR)]
        fq_a = sb.tile([P, PAIR, P, PACK], BF16, align_bytes=64)
        fq_b = [sb.tile([P, P, PACK], BF16, align_bytes=64, name=f"fqb{r}") for r in range(PAIR)]
        codes_a = sb.tile([P, HALF], U32, align_bytes=64)
        scales_a = sb.tile([P, HALF], U8, align_bytes=64)
        codes_b = [sb.tile([P, P], U32, align_bytes=64, name=f"qcb{r}") for r in range(PAIR)]
        scales_b = [sb.tile([P, P], U8, align_bytes=64, name=f"qsb{r}") for r in range(PAIR)]
        y_a = [ps.tile([P, PAIR + 1, E], F32, name=f"ya{h}") for h in range(H)]
        y_last = [ps.tile([P, E], F32, name=f"yl{h}") for h in range(H)]
        y_b = [[y_a[h][:, PAIR, :] for h in range(H)], [y_last[h][:] for h in range(H)]]
        rcp_a = [sb.tile([P, PAIR + 1], F32, name=f"rcpa{h}") for h in range(H)]
        rcp_last = [sb.tile([P, 1], F32, name=f"rcpl{h}") for h in range(H)]
        rcp_b = [[rcp_a[h][:, PAIR:PAIR + 1] for h in range(H)], [rcp_last[h][:] for h in range(H)]]
        res_a = [sb.tile([P, PAIR * E], F32, name=f"resa{h}") for h in range(H)]
        res_b = [sb.tile([P, H, E], F32, name=f"resb{r}") for r in range(PAIR)]
        warm_in = sb.tile([P, 1], F32)
        warm_out = sb.tile([P, 1], F32)

        def load_q(c):
            nc.sync.dma_start(out=q_sb[c][:], in_=q_rows[:, :, c * HALF:(c + 1) * HALF])

        def load_qa(engine):
            for h in range(H):
                engine.dma_start(out=qa_sb[h * ROWS:(h + 1) * ROWS, :], in_=qa.rearrange("(p j) o -> p (j o)", j=PACK))

        def load_s():
            nc.sync.dma_start(out=s_sb[:], in_=S.rearrange("h (p j) e -> (h p) j e", j=PACK))

        def load_og_a():
            nc.sync.dma_start(out=og_a[:], in_=og_a_rows)

        def load_og_b(r):
            nc.sync.dma_start(out=og_b[r][:], in_=og_b_rows[r])

        load_q(0)
        load_qa(nc.sync)
        load_q(1)
        load_s()
        load_og_a()
        load_og_b(0)
        load_og_b(1)

        nc.vector.memset(warm_in[:], 0.0)
        nc.scalar.activation(out=warm_out[:], in_=warm_in[:], func=ACT.Sigmoid)

        def square_a(k):
            first = sum(PIECES[:k])
            cols = q_sb[0][:, :, PAIR * first:PAIR * (first + PIECES[k])]
            nc.scalar.activation(
                out=sq_a[k][:].rearrange("p r m j -> p m j r"),
                in_=cols.rearrange("p j (m r) -> p m j r", r=PAIR),
                func=ACT.Square,
            )

        def square_b(r, lo=0, hi=P):
            nc.scalar.activation(
                out=sq_b[r][:, lo:hi, :].rearrange("p (a i) j -> p a j i", i=PAIR),
                in_=q_sb[1][:, :, r * P + lo:r * P + hi].rearrange("p j (a i) -> p a j i", i=PAIR),
                func=ACT.Square,
            )

        def feature_map(dst, squares, columns):
            nc.vector.scalar_tensor_tensor(
                out=dst,
                in0=squares,
                scalar=0.125,
                in1=qa_sb[:].unsqueeze(1).to_broadcast([P, columns, PACK]),
                op0=ALU.add,
                op1=ALU.mult,
            )

        def map_a(k):
            first = sum(PIECES[:k])
            feature_map(
                fq_a[:, :, first:first + PIECES[k], :].rearrange("p r m j -> p r (m j)"),
                sq_a[k][:].rearrange("p r m j -> p (r m) j"),
                PAIR * PIECES[k],
            )

        def map_b(r, lo=0, hi=P):
            feature_map(fq_b[r][:, lo:hi, :], sq_b[r][:, lo:hi, :], hi - lo)

        def quantize(codes, scales, values):
            nc.vector.quantize_mx(out=codes[:].bitcast(FP8X4), scales=scales[:], in_=values)

        def quantize_a():
            quantize(codes_a, scales_a, fq_a[:].rearrange("p r m j -> p (r m j)"))

        def quantize_b(r):
            quantize(codes_b[r], scales_b[r], fq_b[r][:].rearrange("p m j -> p (m j)"))

        def quantize_s():
            quantize(s_codes, s_scales, s_bf[:].rearrange("p e j -> p (e j)"))

        def multiply(dst, h, codes, scales, cols):
            rows = slice(h * ROWS, (h + 1) * ROWS)
            nc.tensor.matmul_mx(
                out=dst,
                lhsT=codes[rows, cols].bitcast(FP8X4),
                lhsT_scale=scales[rows, cols],
                rhs=s_codes[rows, :].bitcast(FP8X4),
                rhs_scale=s_scales[rows, :],
                start=True,
                stop=True,
            )

        def multiply_a(h):
            for r in range(PAIR):
                multiply(y_a[h][:, r, :], h, codes_a, scales_a, slice(r * P, (r + 1) * P))

        def multiply_b(r, h):
            multiply(y_b[r][h], h, codes_b[r], scales_b[r], slice(0, P))

        def sigmoid_a(h):
            nc.scalar.activation(out=gate_a[:, h, :], in_=og_a[:, h, :], func=ACT.Sigmoid)

        def sigmoid_b(r):
            nc.scalar.activation(out=gate_b[r][:], in_=og_b[r][:], func=ACT.Sigmoid)

        def rcp_of_a(h):
            nc.vector.reciprocal(out=rcp_a[h][:], in_=y_a[h][:, :, E - 1])

        def rcp_of_b(r, h):
            nc.vector.reciprocal(out=rcp_b[r][h], in_=y_b[r][h][:, E - 1:E])

        def finish(dst, sums, rcp, gate):
            nc.vector.scalar_tensor_tensor(out=dst, in0=sums, scalar=rcp, in1=gate, op0=ALU.mult, op1=ALU.mult)

        def finish_a(h, r):
            cols = slice(r * E, (r + 1) * E)
            finish(res_a[h][:, cols], y_a[h][:, r, :], rcp_a[h][:, r:r + 1], gate_a[:, h, cols])

        def finish_b(r, h):
            finish(res_b[r][:, h, :], y_b[r][h], rcp_b[r][h], gate_b[r][:, h, :])

        def store_a(engine, h):
            engine.dma_start(out=out_a_rows[h], in_=res_a[h][:])

        def store_b(r):
            nc.sync.dma_start(out=out_b_rows[r], in_=res_b[r][:])

        def store_b_head(engine, r, h):
            engine.dma_start(out=out_b_rows[r][:, h, :], in_=res_b[r][:, h, :])

        def pack_s(copy):
            copy(
                out=s_bf[:].rearrange("p (a i) j -> p a j i", i=PAIR),
                in_=s_sb[:].rearrange("p j (a i) -> p a j i", i=PAIR),
            )

        square_a(0)
        square_a(1)
        square_a(2)
        square_b(0, 0, 64)
        square_b(0, 64, 128)
        pack_s(nc.scalar.copy)
        square_b(1)
        sigmoid_a(0)
        sigmoid_b(0)
        sigmoid_a(1)
        sigmoid_b(1)
        map_a(0)
        map_a(1)
        map_a(2)
        map_b(0, 0, 64)
        map_b(0, 64, 128)
        quantize_a()
        quantize_s()
        quantize_b(0)
        multiply_a(0)
        multiply_b(0, 0)
        multiply_a(1)
        multiply_b(0, 1)
        map_b(1)
        rcp_of_a(0)
        quantize_b(1)
        multiply_b(1, 0)
        multiply_b(1, 1)
        finish_a(0, 0)
        rcp_of_a(1)
        finish_a(0, 1)
        store_a(nc.sync, 0)
        finish_b(0, 0)
        finish_b(0, 1)
        store_b(0)
        finish_a(1, 0)
        rcp_of_b(1, 0)
        finish_a(1, 1)
        store_a(nc.sync, 1)
        rcp_of_b(1, 1)
        finish_b(1, 0)
        store_b_head(nc.sync, 1, 0)
        finish_b(1, 1)
        store_b_head(nc.scalar, 1, 1)
